import numpy as np
import ml_dtypes


def mxq(x, axis, fmt="e4m3"):
    dtype, down = {"e4m3": (ml_dtypes.float8_e4m3fn, 7), "e5m2": (ml_dtypes.float8_e5m2, 14)}[fmt]
    v = np.moveaxis(np.asarray(x, np.float32).astype(ml_dtypes.bfloat16).astype(np.float64), axis, -1)
    blocks = v.reshape(v.shape[:-1] + (-1, 32))
    amax = np.abs(blocks).max(-1, keepdims=True)
    byte = np.maximum(np.where(amax > 0, np.frexp(amax)[1] - 1 + 127, 0) - down, 1)
    scale = np.exp2(byte - 127.0)
    codes = (blocks / scale).astype(np.float32).astype(dtype).astype(np.float64)
    return np.moveaxis((codes * scale).reshape(v.shape), -1, axis)


WIDE = False


def mx_kscale(k):
    if not WIDE:
        return np.ones(k)
    levels = np.array([10, -10, 5, -5, 0])
    if k % 512:
        return np.exp2(np.random.permutation(np.resize(levels, k // 32))).repeat(32)
    a = np.empty((k // 512, 16))
    for p in range(k // 512):
        a[p, :8] = np.random.permutation(np.resize(levels, 8))
        for g in range(8):
            far = levels[np.abs(levels - a[p, g]) >= 10]
            a[p, g + 8] = far[np.random.randint(len(far))]
    return np.exp2(a.ravel()).repeat(32)


def f64(x):
    return np.asarray(x).astype(np.float64)


def striped(idx):
    return np.tile(idx.reshape(-1, 16).T, (8, 1)).astype(np.uint16)


def unstriped(offs):
    return offs[:16].T.reshape(-1).astype(np.int64)


def pack_weight(w):
    k, n = w.shape
    w = f64(np.asarray(w, np.float32).astype(ml_dtypes.bfloat16)).reshape(k // 32, 32, n)
    amax = np.abs(w).max(1)
    byte = np.clip(np.where(amax > 0, np.frexp(amax)[1] - 1 + 127 - 7, 1), 1, 254)
    scaled = (w * np.exp2(127.0 - byte)[:, None, :]).reshape(k, n).astype(np.float32)
    words = np.ascontiguousarray(scaled.reshape(k // 512, 128, 4, n).transpose(0, 1, 3, 2)).astype(ml_dtypes.float8_e4m3fn).view(np.uint8)
    return words, np.ascontiguousarray(byte.astype(np.uint8).reshape(k // 512, 16, n))


def unpack_weight(words, scales):
    g, p, n, _ = words.shape
    vals = np.ascontiguousarray(words).view(ml_dtypes.float8_e4m3fn).astype(np.float64) * np.repeat(np.exp2(scales.astype(np.float64) - 127.0), 8, axis=1)[..., None]
    return vals.transpose(0, 1, 3, 2).reshape(g * 512, n)


def planes(y):
    n, m = y.shape
    v = y.astype(np.float32).astype(ml_dtypes.bfloat16).astype(np.float64).reshape(n // 32, 32, m)
    top = np.abs(v).max(1)
    byte = np.clip(np.where(top > 0, np.frexp(top)[1] - 1 + 127 - 7, 1), 1, 254)
    codes = (v * np.exp2(127.0 - byte)[:, None, :]).reshape(n, m).astype(np.float32).astype(ml_dtypes.float8_e4m3fn).view(np.uint8)
    words = codes.reshape(n // 512, 128, 4, m).transpose(0, 1, 3, 2)
    return np.ascontiguousarray(words), np.ascontiguousarray(byte.astype(np.uint8).reshape(n // 512, 16, m))


K, T, S, N, H, W = 512, 2048, 512, 512, 512, 1024


def setup_inputs():
    n = np.random.standard_normal
    s = mx_kscale(K)[:, None]
    u = mx_kscale(H)
    packed_xT = pack_weight(n((K, T)) * s)
    packed_eT = pack_weight(n((K, W)) * s)
    return {
        "x_words": packed_xT[0],
        "x_scales": packed_xT[1],
        "w1": (n((K, N)) / np.sqrt(K) / s).astype(np.float32),
        "e_words": packed_eT[0],
        "e_scales": packed_eT[1],
        "w2": (n((K, N)) / np.sqrt(K) / s).astype(np.float32),
        "unit": (np.random.uniform(0.6, 1.4, (H, 1)) * u[:, None]).astype(np.float32),
        "w3": (n((H, N)) / np.sqrt(H) / u[:, None]).astype(np.float32),
        "offs": striped(np.random.permutation(T)[:S]),
        "old1": striped(np.random.permutation(W)[:S]),
        "org": striped(np.random.permutation(S)),
        "sib": striped(np.random.permutation(S)),
    }


def reference(x_words, x_scales, w1, e_words, e_scales, w2, unit, w3, offs, old1, org, sib):
    xq = unpack_weight(x_words, x_scales)[:, unstriped(offs)]
    y = mxq(f64(w1), 0, "e4m3").T @ xq
    e_old1 = unpack_weight(e_words, e_scales)[:, unstriped(old1)]
    ye = mxq(f64(w2), 0, "e4m3").T @ e_old1
    eo = ye[:, unstriped(org)]
    dif = y - (0.7 * eo)
    ds = dif[:, unstriped(sib)]
    hid = f64(unit) * (dif * ds + eo)
    out_0 = mxq(f64(w3), 0, "e4m3").T @ mxq(hid, 0, "e4m3")
    return (out_0,) + planes(out_0)

@@ -1,0 +1,188 @@
+from contextlib import ExitStack
+
+import concourse.mybir as mybir
+
+F32 = mybir.dt.float32
+BF16 = mybir.dt.bfloat16
+I32 = mybir.dt.int32
+U32 = mybir.dt.uint32
+U16 = mybir.dt.uint16
+U8 = mybir.dt.uint8
+FP8X4 = mybir.dt.float8_e4m3fn_x4
+MULT = mybir.AluOpType.mult
+ADD = mybir.AluOpType.add
+IS_EQUAL = mybir.AluOpType.is_equal
+COPY = mybir.ActivationFunctionType.Copy
+
+P = 128
+PACK = 4
+S = 512
+HALF = S // 2
+FLOPS = 3 * 2 * 512 * 512 * 512
+WIDTHS = [256,128,128]
+ENG = {"w2a":"S","w2b":"V","w1a":"S","w1b":"V","w3a":"V","w3b":"S","org10":"V","org11":"V","rnd0":"S","rnd1":"S","cp11":"V","cp20":"V","rnd2":"V"}
+LOADS = ["unitG","old","offs","ew","w2a","es","w2b","org","w1a","xs","w1b","xw","sib","w3a","w3b"]
+
+
+def tile_picked_ycodrev_mul_po_kernel(
+    tc, x_words, x_scales, w1, e_words, e_scales, w2, unit, w3, offs, old1, org, sib, out_0, out_1, out_2
+):
+    nc = tc.nc
+    with ExitStack() as ctx:
+        keep = ctx.enter_context(tc.tile_pool(name="keep", bufs=1))
+        ring = ctx.enter_context(tc.tile_pool(name="ring", bufs=5))
+        psum = ctx.enter_context(tc.psum_pool(name="psum", bufs=1))
+
+        def copy_on(key, out, in_, default):
+            e = ENG.get(key, default)
+            if e == "V":
+                nc.vector.tensor_copy(out, in_)
+            elif e == "S":
+                nc.scalar.copy(out, in_)
+            else:
+                nc.gpsimd.tensor_scalar(out, in_, 1.0, 0.0, MULT, ADD)
+
+        def gather_on(key, out, window):
+            if ENG.get(key, "S") == "V":
+                nc.vector.tensor_copy(out, window)
+            else:
+                nc.scalar.activation(out, window, COPY)
+
+        es = keep.tile([P, 1024], U8, name="e_scale_table")
+        nc.gpsimd.memset(es[:].bitcast(I32), 0)
+        xs = keep.tile([P, 2048], U8, name="x_scale_table")
+        nc.gpsimd.memset(xs[:].bitcast(I32), 0)
+        lists = {"old": old1, "offs": offs, "org": org, "sib": sib}
+        tables = {"ew": e_words, "xw": x_words}
+        planes = {"es": (es, e_scales), "xs": (xs, x_scales)}
+        weights = {"w1": w1, "w2": w2, "w3": w3}
+        sb = {}
+        for key in LOADS:
+            if key in lists:
+                sb[key] = keep.tile([P, S // 16], U16, name=key + "_list")
+                nc.sync.dma_start(sb[key][:], lists[key])
+            elif key in tables:
+                sb[key] = keep.tile([P, tables[key].shape[2]], U32, name=key + "_table")
+                nc.sync.dma_start(sb[key][:].bitcast(I32), tables[key][0].rearrange("p n r -> p (n r)").bitcast(I32))
+            elif key in planes:
+                t, src = planes[key]
+                for q in range(4):
+                    nc.sync.dma_start(t[32 * q : 32 * q + 4, :].bitcast(I32), src[0, 4 * q : 4 * q + 4, :].bitcast(I32))
+            elif key == "unitG":
+                u = keep.tile([P, PACK], F32, name="u")
+                nc.gpsimd.dma_start(u[:], unit.rearrange("(p t) o -> p (t o)", t=PACK))
+            else:
+                h = 0 if key[2] == "a" else 1
+                sb[key] = keep.tile([P, PACK, 256], F32, name=key + "_raw")
+                nc.sync.dma_start(sb[key][:], weights[key[:2]].rearrange("(p j) c -> p j c", j=PACK)[:, :, 256 * h : 256 * h + 256])
+
+        y_gain = keep.tile([P, PACK], F32, name="y_gain")
+        nc.gpsimd.tensor_scalar(y_gain[:], u[:], -1.0 / 0.7, 0.0, MULT, ADD)
+        u_zero = keep.tile([P, PACK], F32, name="u_zero")
+        nc.gpsimd.tensor_scalar(u_zero[:], u[:], 0.0, 1.0, IS_EQUAL, MULT)
+        u_scaled = keep.tile([P, PACK], F32, name="u_scaled")
+        nc.gpsimd.tensor_scalar(u_scaled[:], u[:], 1.0 / (0.7 * 0.7), 0.0, MULT, ADD)
+        divisor = keep.tile([P, PACK], F32, name="divisor")
+        nc.gpsimd.tensor_tensor(divisor[:], u_scaled[:], u_zero[:], ADD)
+        p_gain = keep.tile([P, PACK], F32, name="p_gain")
+        nc.vector.reciprocal(p_gain[:], divisor[:])
+
+        def prepare_weight(name, tag, calls):
+            g = keep.tile([P, PACK, P, PACK], BF16, name=name + "_bf", tag=tag, align_bytes=64)
+            for h in range(2):
+                key = name + "ab"[h]
+                copy_on(
+                    key,
+                    g[:, :, 64 * h : 64 * h + 64, :].rearrange("p t m j -> p m t j"),
+                    sb[key][:].rearrange("p j (m t) -> p m t j", t=PACK),
+                    "V",
+                )
+            codes = keep.tile([P, PACK, P], U32, name=name + "_codes", align_bytes=64)
+            scales = keep.tile([P, PACK, P], U8, name=name + "_scales", align_bytes=64)
+            per = PACK // calls
+            for a in range(0, PACK, per):
+                nc.vector.quantize_mx(
+                    out=codes[:, a : a + per, :].rearrange("p t m -> p (t m)").bitcast(FP8X4),
+                    scales=scales[:, a : a + per, :].rearrange("p t m -> p (t m)"),
+                    in_=g[:, a : a + per, :, :].rearrange("p t m j -> p (t m j)"),
+                )
+            return codes, scales
+
+        e_pw = keep.tile([P, S], U32, name="e_picked_words", align_bytes=64)
+        nc.vector.tensor_copy(e_pw[:], sb["ew"][:].indirect(sb["old"][:]))
+        e_ps = keep.tile([P, S], U8, name="e_picked_scales", align_bytes=64)
+        nc.vector.tensor_copy(e_ps[:], es[:].indirect(sb["old"][:]))
+        w2_codes, w2_scales = prepare_weight("w2", "w2_bf", 2)
+
+        eou = keep.tile([P, PACK, S], F32, name="eou")
+        for t in range(PACK):
+            bank = psum.tile([P, S], F32, name="bank%d" % t)
+            nc.tensor.matmul_mx(bank[:], lhsT=w2_codes[:, t, :].bitcast(FP8X4), lhsT_scale=w2_scales[:, t, :],
+                                rhs=e_pw[:].bitcast(FP8X4), rhs_scale=e_ps[:], start=True, stop=True)
+            yeu = keep.tile([P, S], F32, name="yeu%d" % t)
+            nc.scalar.activation(yeu[:], bank[:], COPY, scale=u[:, t : t + 1])
+            for h in range(2):
+                gather_on("org%d%d" % (t, h), eou[:, t, HALF * h : HALF * h + HALF], yeu[:].indirect(sb["org"][:, 16 * h : 16 * h + 16]))
+
+        x_ps = keep.tile([P, S], U8, name="x_picked_scales", align_bytes=64)
+        nc.vector.tensor_copy(x_ps[:], xs[:].indirect(sb["offs"][:]))
+        x_parts = 1
+        x_width = S // x_parts
+        x_pw = []
+        for h in range(x_parts):
+            part = keep.tile([P, x_width], U32, name="x_picked_words%d" % h, align_bytes=64)
+            nc.vector.tensor_copy(part[:], sb["xw"][:].indirect(sb["offs"][:, h * x_width // 16 : (h + 1) * x_width // 16]))
+            x_pw.append(part)
+        w1_codes, w1_scales = prepare_weight("w1", "w1_bf", 2)
+
+        dif = []
+        for t in range(PACK):
+            bank = psum.tile([P, S], F32, name="bank%d" % (PACK + t))
+            for h in range(x_parts):
+                cols = slice(h * x_width, (h + 1) * x_width)
+                nc.tensor.matmul_mx(bank[:, cols], lhsT=w1_codes[:, t, :].bitcast(FP8X4), lhsT_scale=w1_scales[:, t, :],
+                                    rhs=x_pw[h][:].bitcast(FP8X4), rhs_scale=x_ps[:, cols], start=True, stop=True)
+            d = keep.tile([P, S], F32, name="dif%d" % t)
+            nc.vector.scalar_tensor_tensor(d[:], bank[:], y_gain[:, t : t + 1], eou[:, t, :], MULT, ADD)
+            dif.append(d)
+
+        w3_codes, w3_scales = prepare_weight("w3", "w3_bf", 2)
+
+        out_rows = out_0.rearrange("(p t) j -> p t j", t=PACK)
+        out_words = out_1[0].rearrange("p n r -> p (n r)").bitcast(I32)
+        out_scales = keep.tile([P, S], U8, name="out_scales", align_bytes=64)
+        for c, n in enumerate(WIDTHS):
+            j0 = sum(WIDTHS[:c])
+            prod = keep.tile([P, PACK, n], F32, name="prod%d" % c)
+            for t in range(PACK):
+                ds = ring.tile([P, n], F32, name="ds")
+                gather_on("sib%d%d" % (c, t), ds[:], dif[t][:].indirect(sb["sib"][:, j0 // 16 : (j0 + n) // 16]))
+                nc.vector.scalar_tensor_tensor(prod[:, t, :], dif[t][:, j0 : j0 + n], p_gain[:, t : t + 1], ds[:], MULT, MULT)
+            hid = keep.tile([P, n, PACK], BF16, name="hid%d" % c, align_bytes=64)
+            nc.vector.tensor_tensor(
+                hid[:].rearrange("p (c i) t -> p c t i", i=4),
+                prod[:].rearrange("p t (c i) -> p c t i", i=4),
+                eou[:, :, j0 : j0 + n].rearrange("p t (c i) -> p c t i", i=4),
+                ADD,
+            )
+            hid_codes = keep.tile([P, n], U32, name="hid_codes%d" % c, align_bytes=64)
+            hid_scales = keep.tile([P, n], U8, name="hid_scales%d" % c, align_bytes=64)
+            nc.vector.quantize_mx(out=hid_codes[:].bitcast(FP8X4), scales=hid_scales[:], in_=hid[:].rearrange("p n t -> p (n t)"))
+
+            res = keep.tile([P, PACK, n], F32, name="res%d" % c)
+            for a in range(2):
+                bank = psum.tile([P, 2, n], F32, name="bank%d" % ((2 * c + a) % 4))
+                for v in range(2):
+                    t = 2 * a + v
+                    nc.tensor.matmul_mx(bank[:, v, :], lhsT=w3_codes[:, t, :].bitcast(FP8X4), lhsT_scale=w3_scales[:, t, :],
+                                        rhs=hid_codes[:].bitcast(FP8X4), rhs_scale=hid_scales[:], start=True, stop=True)
+                copy_on("cp%d%d" % (c, a), res[:, 2 * a : 2 * a + 2, :], bank[:], "S")
+            nc.sync.dma_start(out_rows[:, :, j0 : j0 + n], res[:])
+            res_bf = keep.tile([P, n, PACK], BF16, name="res_bf%d" % c, align_bytes=64)
+            copy_on("rnd%d" % c, res_bf[:].rearrange("p (c i) t -> p c t i", i=4), res[:].rearrange("p t (c i) -> p c t i", i=4), "V")
+            res_codes = keep.tile([P, n], U32, name="res_codes%d" % c, align_bytes=64)
+            nc.vector.quantize_mx(out=res_codes[:].bitcast(FP8X4), scales=out_scales[:, j0 : j0 + n], in_=res_bf[:].rearrange("p n t -> p (n t)"))
+            nc.sync.dma_start(out_words[:, j0 : j0 + n], res_codes[:].bitcast(I32))
+        for q in range(4):
+            queue = nc.sync if q % 2 == 0 else nc.scalar
+            queue.dma_start(out_2[0, 4 * q : 4 * q + 4, :].bitcast(I32), out_scales[32 * q : 32 * q + 4, :].bitcast(I32))

@@ -20,8 +20,8 @@ S = 512
 HALF = S // 2
 FLOPS = 3 * 2 * 512 * 512 * 512
 WIDTHS = [256,128,128]
-ENG = {"w2a":"S","w2b":"V","w1a":"S","w1b":"V","w3a":"V","w3b":"S","org10":"V","org11":"V","rnd0":"S","rnd1":"S","cp11":"V","cp20":"V","rnd2":"V"}
-LOADS = ["unitG","old","offs","ew","w2a","es","w2b","org","w1a","xs","w1b","xw","sib","w3a","w3b"]
+ENG = {"w2a":"S","w2b":"V","w1a":"S","w1b":"V","w3a":"V","w3b":"V","org11":"V","org21":"V","rnd0":"S","rnd1":"S","cp11":"V","cp20":"V","rnd2":"V"}
+LOADS = ["old","unit","ew","w2a","es","w2b","offs","w1a","xs","w1b","org","xw","sib","w3a","w3b"]
 
 
 def tile_picked_ycodrev_mul_po_kernel(
@@ -30,7 +30,7 @@ def tile_picked_ycodrev_mul_po_kernel(
     nc = tc.nc
     with ExitStack() as ctx:
         keep = ctx.enter_context(tc.tile_pool(name="keep", bufs=1))
-        ring = ctx.enter_context(tc.tile_pool(name="ring", bufs=5))
+        ring = ctx.enter_context(tc.tile_pool(name="ring", bufs=6))
         psum = ctx.enter_context(tc.psum_pool(name="psum", bufs=1))
 
         def copy_on(key, out, in_, default):
@@ -68,24 +68,13 @@ def tile_picked_ycodrev_mul_po_kernel(
                 t, src = planes[key]
                 for q in range(4):
                     nc.sync.dma_start(t[32 * q : 32 * q + 4, :].bitcast(I32), src[0, 4 * q : 4 * q + 4, :].bitcast(I32))
-            elif key == "unitG":
+            elif key == "unit":
                 u = keep.tile([P, PACK], F32, name="u")
-                nc.gpsimd.dma_start(u[:], unit.rearrange("(p t) o -> p (t o)", t=PACK))
+                nc.sync.dma_start(u[:], unit.rearrange("(p t) o -> p (t o)", t=PACK))
             else:
                 h = 0 if key[2] == "a" else 1
                 sb[key] = keep.tile([P, PACK, 256], F32, name=key + "_raw")
                 nc.sync.dma_start(sb[key][:], weights[key[:2]].rearrange("(p j) c -> p j c", j=PACK)[:, :, 256 * h : 256 * h + 256])
-
-        y_gain = keep.tile([P, PACK], F32, name="y_gain")
-        nc.gpsimd.tensor_scalar(y_gain[:], u[:], -1.0 / 0.7, 0.0, MULT, ADD)
-        u_zero = keep.tile([P, PACK], F32, name="u_zero")
-        nc.gpsimd.tensor_scalar(u_zero[:], u[:], 0.0, 1.0, IS_EQUAL, MULT)
-        u_scaled = keep.tile([P, PACK], F32, name="u_scaled")
-        nc.gpsimd.tensor_scalar(u_scaled[:], u[:], 1.0 / (0.7 * 0.7), 0.0, MULT, ADD)
-        divisor = keep.tile([P, PACK], F32, name="divisor")
-        nc.gpsimd.tensor_tensor(divisor[:], u_scaled[:], u_zero[:], ADD)
-        p_gain = keep.tile([P, PACK], F32, name="p_gain")
-        nc.vector.reciprocal(p_gain[:], divisor[:])
 
         def prepare_weight(name, tag, calls):
             g = keep.tile([P, PACK, P, PACK], BF16, name=name + "_bf", tag=tag, align_bytes=64)
@@ -124,9 +113,18 @@ def tile_picked_ycodrev_mul_po_kernel(
             for h in range(2):
                 gather_on("org%d%d" % (t, h), eou[:, t, HALF * h : HALF * h + HALF], yeu[:].indirect(sb["org"][:, 16 * h : 16 * h + 16]))
 
+        y_gain = keep.tile([P, PACK], F32, name="y_gain")
+        nc.vector.tensor_scalar(y_gain[:], u[:], -1.0 / 0.7, None, MULT)
+        u_zero = keep.tile([P, PACK], F32, name="u_zero")
+        nc.vector.tensor_scalar(u_zero[:], u[:], 0.0, None, IS_EQUAL)
+        divisor = keep.tile([P, PACK], F32, name="divisor")
+        nc.vector.scalar_tensor_tensor(divisor[:], u[:], 1.0 / (0.7 * 0.7), u_zero[:], MULT, ADD)
+        p_gain = keep.tile([P, PACK], F32, name="p_gain")
+        nc.vector.reciprocal(p_gain[:], divisor[:])
+
         x_ps = keep.tile([P, S], U8, name="x_picked_scales", align_bytes=64)
         nc.vector.tensor_copy(x_ps[:], xs[:].indirect(sb["offs"][:]))
-        x_parts = 1
+        x_parts = 2
         x_width = S // x_parts
         x_pw = []
         for h in range(x_parts):

@@ -54,7 +54,7 @@ def tile_picked_ycodrev_mul_po_kernel(
         nc.gpsimd.memset(xs[:].bitcast(I32), 0)
         lists = {"old": old1, "offs": offs, "org": org, "sib": sib}
         tables = {"ew": e_words, "xw": x_words}
-        planes = {"es": (es, e_scales), "xs": (xs, x_scales)}
+        planes = {"es": (es, e_scales, 0), "xs": (xs, x_scales, 4)}
         weights = {"w1": w1, "w2": w2, "w3": w3}
         sb = {}
         for key in LOADS:
@@ -65,9 +65,9 @@ def tile_picked_ycodrev_mul_po_kernel(
                 sb[key] = keep.tile([P, tables[key].shape[2]], U32, name=key + "_table")
                 nc.sync.dma_start(sb[key][:].bitcast(I32), tables[key][0].rearrange("p n r -> p (n r)").bitcast(I32))
             elif key in planes:
-                t, src = planes[key]
-                for q in range(4):
-                    nc.sync.dma_start(t[32 * q : 32 * q + 4, :].bitcast(I32), src[0, 4 * q : 4 * q + 4, :].bitcast(I32))
+                t, src, first = planes[key]
+                for r in range(4):
+                    nc.sync.dma_start(t[first + r : P : 32, :].bitcast(I32), src[0, r:16:4, :].bitcast(I32))
             elif key == "unit":
                 u = keep.tile([P, PACK], F32, name="u")
                 nc.sync.dma_start(u[:], unit.rearrange("(p t) o -> p (t o)", t=PACK))
@@ -139,7 +139,7 @@ def tile_picked_ycodrev_mul_po_kernel(
             for h in range(x_parts):
                 cols = slice(h * x_width, (h + 1) * x_width)
                 nc.tensor.matmul_mx(bank[:, cols], lhsT=w1_codes[:, t, :].bitcast(FP8X4), lhsT_scale=w1_scales[:, t, :],
-                                    rhs=x_pw[h][:].bitcast(FP8X4), rhs_scale=x_ps[:, cols], start=True, stop=True)
+                                    rhs=x_pw[h][:].bitcast(FP8X4), rhs_scale=x_ps[4:P, cols], start=True, stop=True)
             d = keep.tile([P, S], F32, name="dif%d" % t)
             nc.vector.scalar_tensor_tensor(d[:], bank[:], y_gain[:, t : t + 1], eou[:, t, :], MULT, ADD)
             dif.append(d)
@@ -183,4 +183,4 @@ def tile_picked_ycodrev_mul_po_kernel(
             nc.sync.dma_start(out_words[:, j0 : j0 + n], res_codes[:].bitcast(I32))
         for q in range(4):
             queue = nc.sync if q % 2 == 0 else nc.scalar
-            queue.dma_start(out_2[0, 4 * q : 4 * q + 4, :].bitcast(I32), out_scales[32 * q : 32 * q + 4, :].bitcast(I32))
+            queue.dma_start(out_2[0, q:16:4, :].bitcast(I32), out_scales[q:P:32, :].bitcast(I32))

@@ -14,14 +14,21 @@ ADD = mybir.AluOpType.add
 IS_EQUAL = mybir.AluOpType.is_equal
 COPY = mybir.ActivationFunctionType.Copy
 
+FLOPS = 3 * 2 * 512 * 512 * 512
+
 P = 128
 PACK = 4
 S = 512
 HALF = S // 2
-FLOPS = 3 * 2 * 512 * 512 * 512
-WIDTHS = [256,128,128]
-ENG = {"w2a":"S","w2b":"V","w1a":"S","w1b":"V","w3a":"V","w3b":"V","org11":"V","org21":"V","rnd0":"S","rnd1":"S","cp11":"V","cp20":"V","rnd2":"V"}
-LOADS = ["old","unit","ew","w2a","es","w2b","offs","w1a","xs","w1b","org","xw","sib","w3a","w3b"]
+QUARTER = S // 4
+PER_COLUMN = 16
+SCALE_ROWS = 16
+QUADRANT = 32
+X_PLANE = 4
+LOSS = 0.7
+M_HALF = P // 2
+W2_VECTOR_M = 40
+SIBLING_BUFS = PACK
 
 
 def tile_picked_ycodrev_mul_po_kernel(
@@ -30,157 +37,180 @@ def tile_picked_ycodrev_mul_po_kernel(
     nc = tc.nc
     with ExitStack() as ctx:
         keep = ctx.enter_context(tc.tile_pool(name="keep", bufs=1))
-        ring = ctx.enter_context(tc.tile_pool(name="ring", bufs=6))
+        ring = ctx.enter_context(tc.tile_pool(name="ring", bufs=SIBLING_BUFS))
         psum = ctx.enter_context(tc.psum_pool(name="psum", bufs=1))
 
-        def copy_on(key, out, in_, default):
-            e = ENG.get(key, default)
-            if e == "V":
-                nc.vector.tensor_copy(out, in_)
-            elif e == "S":
-                nc.scalar.copy(out, in_)
-            else:
-                nc.gpsimd.tensor_scalar(out, in_, 1.0, 0.0, MULT, ADD)
+        def load_list(name, src):
+            tile = keep.tile([P, S // PER_COLUMN], U16, name=name)
+            nc.sync.dma_start(tile[:], src)
+            return tile
 
-        def gather_on(key, out, window):
-            if ENG.get(key, "S") == "V":
-                nc.vector.tensor_copy(out, window)
-            else:
-                nc.scalar.activation(out, window, COPY)
+        def load_words(name, src):
+            tile = keep.tile([P, src.shape[2]], U32, name=name, align_bytes=64)
+            nc.sync.dma_start(tile[:].bitcast(I32), src[0].rearrange("p n r -> p (n r)").bitcast(I32))
+            return tile
 
-        es = keep.tile([P, 1024], U8, name="e_scale_table")
-        nc.gpsimd.memset(es[:].bitcast(I32), 0)
-        xs = keep.tile([P, 2048], U8, name="x_scale_table")
-        nc.gpsimd.memset(xs[:].bitcast(I32), 0)
-        lists = {"old": old1, "offs": offs, "org": org, "sib": sib}
-        tables = {"ew": e_words, "xw": x_words}
-        planes = {"es": (es, e_scales, 0), "xs": (xs, x_scales, 4)}
-        weights = {"w1": w1, "w2": w2, "w3": w3}
-        sb = {}
-        for key in LOADS:
-            if key in lists:
-                sb[key] = keep.tile([P, S // 16], U16, name=key + "_list")
-                nc.sync.dma_start(sb[key][:], lists[key])
-            elif key in tables:
-                sb[key] = keep.tile([P, tables[key].shape[2]], U32, name=key + "_table")
-                nc.sync.dma_start(sb[key][:].bitcast(I32), tables[key][0].rearrange("p n r -> p (n r)").bitcast(I32))
-            elif key in planes:
-                t, src, first = planes[key]
-                for r in range(4):
-                    nc.sync.dma_start(t[first + r : P : 32, :].bitcast(I32), src[0, r:16:4, :].bitcast(I32))
-            elif key == "unit":
-                u = keep.tile([P, PACK], F32, name="u")
-                nc.sync.dma_start(u[:], unit.rearrange("(p t) o -> p (t o)", t=PACK))
-            else:
-                h = 0 if key[2] == "a" else 1
-                sb[key] = keep.tile([P, PACK, 256], F32, name=key + "_raw")
-                nc.sync.dma_start(sb[key][:], weights[key[:2]].rearrange("(p j) c -> p j c", j=PACK)[:, :, 256 * h : 256 * h + 256])
+        def cleared_scale_table(name, src):
+            tile = keep.tile([P, src.shape[2]], U8, name=name)
+            nc.gpsimd.memset(tile[:].bitcast(I32), 0)
+            return tile
 
-        def prepare_weight(name, tag, calls):
-            g = keep.tile([P, PACK, P, PACK], BF16, name=name + "_bf", tag=tag, align_bytes=64)
-            for h in range(2):
-                key = name + "ab"[h]
-                copy_on(
-                    key,
-                    g[:, :, 64 * h : 64 * h + 64, :].rearrange("p t m j -> p m t j"),
-                    sb[key][:].rearrange("p j (m t) -> p m t j", t=PACK),
-                    "V",
-                )
+        def load_scales(tile, src, first_row):
+            for r in range(PACK):
+                nc.sync.dma_start(tile[first_row + r : P : QUADRANT, :].bitcast(I32), src[0, r:SCALE_ROWS:PACK, :].bitcast(I32))
+
+        def load_weight_half(name, src, h):
+            tile = keep.tile([P, PACK, HALF], F32, name=name)
+            nc.sync.dma_start(tile[:], src.rearrange("(p j) c -> p j c", j=PACK)[:, :, HALF * h : HALF * (h + 1)])
+            return tile
+
+        def dealt(staged, raw, h):
+            dst = staged[:, :, M_HALF * h : M_HALF * (h + 1), :].rearrange("p t m j -> p m t j")
+            return dst, raw[:].rearrange("p j (m t) -> p m t j", t=PACK)
+
+        def round_on_gpsimd(dst, src):
+            nc.gpsimd.tensor_scalar(dst, src, 1.0, 0.0, MULT, ADD)
+
+        def quantize_weight(name, staged):
             codes = keep.tile([P, PACK, P], U32, name=name + "_codes", align_bytes=64)
             scales = keep.tile([P, PACK, P], U8, name=name + "_scales", align_bytes=64)
-            per = PACK // calls
-            for a in range(0, PACK, per):
+            for t in range(0, PACK, 2):
                 nc.vector.quantize_mx(
-                    out=codes[:, a : a + per, :].rearrange("p t m -> p (t m)").bitcast(FP8X4),
-                    scales=scales[:, a : a + per, :].rearrange("p t m -> p (t m)"),
-                    in_=g[:, a : a + per, :, :].rearrange("p t m j -> p (t m j)"),
+                    out=codes[:, t : t + 2, :].rearrange("p t m -> p (t m)").bitcast(FP8X4),
+                    scales=scales[:, t : t + 2, :].rearrange("p t m -> p (t m)"),
+                    in_=staged[:, t : t + 2, :, :].rearrange("p t m j -> p (t m j)"),
                 )
             return codes, scales
 
-        e_pw = keep.tile([P, S], U32, name="e_picked_words", align_bytes=64)
-        nc.vector.tensor_copy(e_pw[:], sb["ew"][:].indirect(sb["old"][:]))
-        e_ps = keep.tile([P, S], U8, name="e_picked_scales", align_bytes=64)
-        nc.vector.tensor_copy(e_ps[:], es[:].indirect(sb["old"][:]))
-        w2_codes, w2_scales = prepare_weight("w2", "w2_bf", 2)
+        def product(out, weight, t, words, scales):
+            codes, weight_scales = weight
+            nc.tensor.matmul_mx(
+                out,
+                lhsT=codes[:, t, :].bitcast(FP8X4),
+                lhsT_scale=weight_scales[:, t, :],
+                rhs=words.bitcast(FP8X4),
+                rhs_scale=scales,
+                start=True,
+                stop=True,
+            )
+
+        def entries(lst, h):
+            return lst[:, HALF * h // PER_COLUMN : HALF * (h + 1) // PER_COLUMN]
+
+        def planes_of(ap):
+            return ap.rearrange("p t (c i) -> p c t i", i=PACK)
+
+        def words_of(ap):
+            return ap.rearrange("p (c i) t -> p c t i", i=PACK)
+
+        e_scale_table = cleared_scale_table("e_scale_table", e_scales)
+        x_scale_table = cleared_scale_table("x_scale_table", x_scales)
+        old_list = load_list("old_list", old1)
+        u = keep.tile([P, PACK], F32, name="u")
+        nc.sync.dma_start(u[:], unit.rearrange("(p t) o -> p (t o)", t=PACK))
+        e_word_table = load_words("e_word_table", e_words)
+        w2_first = load_weight_half("w2_first", w2, 0)
+        load_scales(e_scale_table, e_scales, 0)
+        w2_second = load_weight_half("w2_second", w2, 1)
+        offs_list = load_list("offs_list", offs)
+        w1_first = load_weight_half("w1_first", w1, 0)
+        load_scales(x_scale_table, x_scales, X_PLANE)
+        w1_second = load_weight_half("w1_second", w1, 1)
+        org_list = load_list("org_list", org)
+        x_word_table = load_words("x_word_table", x_words)
+        sib_list = load_list("sib_list", sib)
+        w3_first = load_weight_half("w3_first", w3, 0)
+        w3_second = load_weight_half("w3_second", w3, 1)
+
+        e_picked_words = keep.tile([P, S], U32, name="e_picked_words", align_bytes=64)
+        nc.vector.tensor_copy(e_picked_words[:], e_word_table[:].indirect(old_list[:]))
+        e_picked_scales = keep.tile([P, S], U8, name="e_picked_scales", align_bytes=64)
+        nc.vector.tensor_copy(e_picked_scales[:], e_scale_table[:].indirect(old_list[:]))
+        w2_staged = keep.tile([P, PACK, P, PACK], BF16, name="w2_staged", align_bytes=64)
+        nc.scalar.copy(*dealt(w2_staged, w2_first, 0))
+        dst, src = dealt(w2_staged, w2_second, 1)
+        nc.scalar.copy(dst[:, W2_VECTOR_M:M_HALF], src[:, W2_VECTOR_M:M_HALF])
+        nc.vector.tensor_copy(dst[:, 0:W2_VECTOR_M], src[:, 0:W2_VECTOR_M])
+        w2_mx = quantize_weight("w2", w2_staged)
 
         eou = keep.tile([P, PACK, S], F32, name="eou")
+        yeu = []
         for t in range(PACK):
             bank = psum.tile([P, S], F32, name="bank%d" % t)
-            nc.tensor.matmul_mx(bank[:], lhsT=w2_codes[:, t, :].bitcast(FP8X4), lhsT_scale=w2_scales[:, t, :],
-                                rhs=e_pw[:].bitcast(FP8X4), rhs_scale=e_ps[:], start=True, stop=True)
-            yeu = keep.tile([P, S], F32, name="yeu%d" % t)
-            nc.scalar.activation(yeu[:], bank[:], COPY, scale=u[:, t : t + 1])
+            product(bank[:], w2_mx, t, e_picked_words[:], e_picked_scales[:])
+            yeu.append(keep.tile([P, S], F32, name="yeu%d" % t))
+            nc.scalar.activation(yeu[t][:], bank[:], COPY, scale=u[:, t : t + 1])
+        for t in range(PACK):
             for h in range(2):
-                gather_on("org%d%d" % (t, h), eou[:, t, HALF * h : HALF * h + HALF], yeu[:].indirect(sb["org"][:, 16 * h : 16 * h + 16]))
+                picked = yeu[t][:].indirect(entries(org_list, h))
+                if t == 0:
+                    nc.vector.tensor_copy(eou[:, t, HALF * h : HALF * (h + 1)], picked)
+                else:
+                    nc.scalar.activation(eou[:, t, HALF * h : HALF * (h + 1)], picked, COPY)
 
         y_gain = keep.tile([P, PACK], F32, name="y_gain")
-        nc.vector.tensor_scalar(y_gain[:], u[:], -1.0 / 0.7, None, MULT)
-        u_zero = keep.tile([P, PACK], F32, name="u_zero")
-        nc.vector.tensor_scalar(u_zero[:], u[:], 0.0, None, IS_EQUAL)
+        nc.vector.tensor_scalar(y_gain[:], u[:], -1.0 / LOSS, None, MULT)
+        u_is_zero = keep.tile([P, PACK], F32, name="u_is_zero")
+        nc.vector.tensor_scalar(u_is_zero[:], u[:], 0.0, None, IS_EQUAL)
         divisor = keep.tile([P, PACK], F32, name="divisor")
-        nc.vector.scalar_tensor_tensor(divisor[:], u[:], 1.0 / (0.7 * 0.7), u_zero[:], MULT, ADD)
-        p_gain = keep.tile([P, PACK], F32, name="p_gain")
-        nc.vector.reciprocal(p_gain[:], divisor[:])
+        nc.vector.scalar_tensor_tensor(divisor[:], u[:], 1.0 / (LOSS * LOSS), u_is_zero[:], MULT, ADD)
+        prod_gain = keep.tile([P, PACK], F32, name="prod_gain")
+        nc.vector.reciprocal(prod_gain[:], divisor[:])
 
-        x_ps = keep.tile([P, S], U8, name="x_picked_scales", align_bytes=64)
-        nc.vector.tensor_copy(x_ps[:], xs[:].indirect(sb["offs"][:]))
-        x_parts = 2
-        x_width = S // x_parts
-        x_pw = []
-        for h in range(x_parts):
-            part = keep.tile([P, x_width], U32, name="x_picked_words%d" % h, align_bytes=64)
-            nc.vector.tensor_copy(part[:], sb["xw"][:].indirect(sb["offs"][:, h * x_width // 16 : (h + 1) * x_width // 16]))
-            x_pw.append(part)
-        w1_codes, w1_scales = prepare_weight("w1", "w1_bf", 2)
+        x_picked_scales = keep.tile([P, S], U8, name="x_picked_scales", align_bytes=64)
+        nc.vector.tensor_copy(x_picked_scales[:], x_scale_table[:].indirect(offs_list[:]))
+        x_picked_words = keep.tile([P, S], U32, name="x_picked_words", align_bytes=64)
+        nc.vector.tensor_copy(x_picked_words[:], x_word_table[:].indirect(offs_list[:]))
+        w1_staged = keep.tile([P, PACK, P, PACK], BF16, name="w1_staged", align_bytes=64)
+        nc.vector.tensor_copy(*dealt(w1_staged, w1_first, 0))
+        round_on_gpsimd(*dealt(w1_staged, w1_second, 1))
+        w1_mx = quantize_weight("w1", w1_staged)
 
-        dif = []
+        w3_staged = keep.tile([P, PACK, P, PACK], BF16, name="w3_staged", tag="x_word_table", align_bytes=64)
+        nc.vector.tensor_copy(*dealt(w3_staged, w3_first, 0))
+        d = keep.tile([P, PACK, S], F32, name="d", tag="w3_first")
         for t in range(PACK):
             bank = psum.tile([P, S], F32, name="bank%d" % (PACK + t))
-            for h in range(x_parts):
-                cols = slice(h * x_width, (h + 1) * x_width)
-                nc.tensor.matmul_mx(bank[:, cols], lhsT=w1_codes[:, t, :].bitcast(FP8X4), lhsT_scale=w1_scales[:, t, :],
-                                    rhs=x_pw[h][:].bitcast(FP8X4), rhs_scale=x_ps[4:P, cols], start=True, stop=True)
-            d = keep.tile([P, S], F32, name="dif%d" % t)
-            nc.vector.scalar_tensor_tensor(d[:], bank[:], y_gain[:, t : t + 1], eou[:, t, :], MULT, ADD)
-            dif.append(d)
-
-        w3_codes, w3_scales = prepare_weight("w3", "w3_bf", 2)
+            product(bank[:], w1_mx, t, x_picked_words[:], x_picked_scales[X_PLANE:P, :])
+            nc.vector.scalar_tensor_tensor(d[:, t, :], bank[:], y_gain[:, t : t + 1], eou[:, t, :], MULT, ADD)
+        round_on_gpsimd(*dealt(w3_staged, w3_second, 1))
+        w3_mx = quantize_weight("w3", w3_staged)
 
         out_rows = out_0.rearrange("(p t) j -> p t j", t=PACK)
         out_words = out_1[0].rearrange("p n r -> p (n r)").bitcast(I32)
         out_scales = keep.tile([P, S], U8, name="out_scales", align_bytes=64)
-        for c, n in enumerate(WIDTHS):
-            j0 = sum(WIDTHS[:c])
-            prod = keep.tile([P, PACK, n], F32, name="prod%d" % c)
+        for h in range(2):
+            half_cols = slice(HALF * h, HALF * (h + 1))
+            prod = keep.tile([P, PACK, HALF], F32, name="prod%d" % h, tag="x_word_table" if h == 0 else "prod_second", align_bytes=64)
             for t in range(PACK):
-                ds = ring.tile([P, n], F32, name="ds")
-                gather_on("sib%d%d" % (c, t), ds[:], dif[t][:].indirect(sb["sib"][:, j0 // 16 : (j0 + n) // 16]))
-                nc.vector.scalar_tensor_tensor(prod[:, t, :], dif[t][:, j0 : j0 + n], p_gain[:, t : t + 1], ds[:], MULT, MULT)
-            hid = keep.tile([P, n, PACK], BF16, name="hid%d" % c, align_bytes=64)
-            nc.vector.tensor_tensor(
-                hid[:].rearrange("p (c i) t -> p c t i", i=4),
-                prod[:].rearrange("p t (c i) -> p c t i", i=4),
-                eou[:, :, j0 : j0 + n].rearrange("p t (c i) -> p c t i", i=4),
-                ADD,
-            )
-            hid_codes = keep.tile([P, n], U32, name="hid_codes%d" % c, align_bytes=64)
-            hid_scales = keep.tile([P, n], U8, name="hid_scales%d" % c, align_bytes=64)
-            nc.vector.quantize_mx(out=hid_codes[:].bitcast(FP8X4), scales=hid_scales[:], in_=hid[:].rearrange("p n t -> p (n t)"))
+                sibling = ring.tile([P, HALF], F32, name="sibling")
+                nc.scalar.activation(sibling[:], d[:, t, :].indirect(entries(sib_list, h)), COPY)
+                nc.vector.scalar_tensor_tensor(prod[:, t, :], d[:, t, half_cols], prod_gain[:, t : t + 1], sibling[:], MULT, MULT)
 
-            res = keep.tile([P, PACK, n], F32, name="res%d" % c)
-            for a in range(2):
-                bank = psum.tile([P, 2, n], F32, name="bank%d" % ((2 * c + a) % 4))
-                for v in range(2):
-                    t = 2 * a + v
-                    nc.tensor.matmul_mx(bank[:, v, :], lhsT=w3_codes[:, t, :].bitcast(FP8X4), lhsT_scale=w3_scales[:, t, :],
-                                        rhs=hid_codes[:].bitcast(FP8X4), rhs_scale=hid_scales[:], start=True, stop=True)
-                copy_on("cp%d%d" % (c, a), res[:, 2 * a : 2 * a + 2, :], bank[:], "S")
-            nc.sync.dma_start(out_rows[:, :, j0 : j0 + n], res[:])
-            res_bf = keep.tile([P, n, PACK], BF16, name="res_bf%d" % c, align_bytes=64)
-            copy_on("rnd%d" % c, res_bf[:].rearrange("p (c i) t -> p c t i", i=4), res[:].rearrange("p t (c i) -> p c t i", i=4), "V")
-            res_codes = keep.tile([P, n], U32, name="res_codes%d" % c, align_bytes=64)
-            nc.vector.quantize_mx(out=res_codes[:].bitcast(FP8X4), scales=out_scales[:, j0 : j0 + n], in_=res_bf[:].rearrange("p n t -> p (n t)"))
-            nc.sync.dma_start(out_words[:, j0 : j0 + n], res_codes[:].bitcast(I32))
-        for q in range(4):
-            queue = nc.sync if q % 2 == 0 else nc.scalar
-            queue.dma_start(out_2[0, q:16:4, :].bitcast(I32), out_scales[q:P:32, :].bitcast(I32))
+            for step in range(2 * h, 2 * h + 2):
+                cols = slice(QUARTER * step, QUARTER * (step + 1))
+                cols_in_half = slice(cols.start - half_cols.start, cols.stop - half_cols.start)
+                hid = keep.tile([P, QUARTER, PACK], BF16, name="hid", align_bytes=64)
+                nc.vector.tensor_tensor(words_of(hid[:]), planes_of(prod[:, :, cols_in_half]), planes_of(eou[:, :, cols]), ADD)
+                hid_codes = keep.tile([P, QUARTER], U32, name="hid_codes%d" % step, align_bytes=64)
+                hid_scales = keep.tile([P, QUARTER], U8, name="hid_scales%d" % step, align_bytes=64)
+                nc.vector.quantize_mx(out=hid_codes[:].bitcast(FP8X4), scales=hid_scales[:], in_=hid[:].rearrange("p n t -> p (n t)"))
+
+                result = keep.tile([P, PACK, QUARTER], F32, name="result%d" % step)
+                for pair in range(2):
+                    bank = psum.tile([P, 2, QUARTER], F32, name="bank%d" % ((2 * step + pair) % PACK))
+                    for v in range(2):
+                        product(bank[:, v, :], w3_mx, 2 * pair + v, hid_codes[:], hid_scales[:])
+                    nc.scalar.copy(result[:, 2 * pair : 2 * pair + 2, :], bank[:])
+                nc.sync.dma_start(out_rows[:, :, cols], result[:])
+
+                rounded = keep.tile([P, QUARTER, PACK], BF16, name="rounded%d" % step, align_bytes=64)
+                round_result = nc.scalar.copy if h == 0 else nc.vector.tensor_copy
+                round_result(words_of(rounded[:]), planes_of(result[:]))
+                result_codes = keep.tile([P, QUARTER], U32, name="result_codes%d" % step, align_bytes=64)
+                nc.vector.quantize_mx(out=result_codes[:].bitcast(FP8X4), scales=out_scales[:, cols], in_=rounded[:].rearrange("p n t -> p (n t)"))
+                nc.sync.dma_start(out_words[:, cols], result_codes[:].bitcast(I32))
+
+        for r in range(PACK):
+            queue = nc.sync if r % 2 == 0 else nc.scalar
+            queue.dma_start(out_2[0, r:SCALE_ROWS:PACK, :].bitcast(I32), out_scales[r:P:QUADRANT, :].bitcast(I32))

from contextlib import ExitStack

import concourse.mybir as mybir

F32 = mybir.dt.float32
BF16 = mybir.dt.bfloat16
I32 = mybir.dt.int32
U32 = mybir.dt.uint32
U16 = mybir.dt.uint16
U8 = mybir.dt.uint8
FP8X4 = mybir.dt.float8_e4m3fn_x4
MULT = mybir.AluOpType.mult
ADD = mybir.AluOpType.add
IS_EQUAL = mybir.AluOpType.is_equal
COPY = mybir.ActivationFunctionType.Copy

FLOPS = 3 * 2 * 512 * 512 * 512

P = 128
PACK = 4
S = 512
HALF = S // 2
QUARTER = S // 4
PER_COLUMN = 16
SCALE_ROWS = 16
QUADRANT = 32
X_PLANE = 4
LOSS = 0.7
M_HALF = P // 2
W2_VECTOR_M = 40
SIBLING_BUFS = PACK


def tile_picked_ycodrev_mul_po_kernel(
    tc, x_words, x_scales, w1, e_words, e_scales, w2, unit, w3, offs, old1, org, sib, out_0, out_1, out_2
):
    nc = tc.nc
    with ExitStack() as ctx:
        keep = ctx.enter_context(tc.tile_pool(name="keep", bufs=1))
        ring = ctx.enter_context(tc.tile_pool(name="ring", bufs=SIBLING_BUFS))
        psum = ctx.enter_context(tc.psum_pool(name="psum", bufs=1))

        def load_list(name, src):
            tile = keep.tile([P, S // PER_COLUMN], U16, name=name)
            nc.sync.dma_start(tile[:], src)
            return tile

        def load_words(name, src):
            tile = keep.tile([P, src.shape[2]], U32, name=name, align_bytes=64)
            nc.sync.dma_start(tile[:].bitcast(I32), src[0].rearrange("p n r -> p (n r)").bitcast(I32))
            return tile

        def cleared_scale_table(name, src):
            tile = keep.tile([P, src.shape[2]], U8, name=name)
            nc.gpsimd.memset(tile[:].bitcast(I32), 0)
            return tile

        def load_scales(tile, src, first_row):
            for r in range(PACK):
                nc.sync.dma_start(tile[first_row + r : P : QUADRANT, :].bitcast(I32), src[0, r:SCALE_ROWS:PACK, :].bitcast(I32))

        def load_weight_half(name, src, h):
            tile = keep.tile([P, PACK, HALF], F32, name=name)
            nc.sync.dma_start(tile[:], src.rearrange("(p j) c -> p j c", j=PACK)[:, :, HALF * h : HALF * (h + 1)])
            return tile

        def dealt(staged, raw, h):
            dst = staged[:, :, M_HALF * h : M_HALF * (h + 1), :].rearrange("p t m j -> p m t j")
            return dst, raw[:].rearrange("p j (m t) -> p m t j", t=PACK)

        def round_on_gpsimd(dst, src):
            nc.gpsimd.tensor_scalar(dst, src, 1.0, 0.0, MULT, ADD)

        def quantize_weight(name, staged):
            codes = keep.tile([P, PACK, P], U32, name=name + "_codes", align_bytes=64)
            scales = keep.tile([P, PACK, P], U8, name=name + "_scales", align_bytes=64)
            for t in range(0, PACK, 2):
                nc.vector.quantize_mx(
                    out=codes[:, t : t + 2, :].rearrange("p t m -> p (t m)").bitcast(FP8X4),
                    scales=scales[:, t : t + 2, :].rearrange("p t m -> p (t m)"),
                    in_=staged[:, t : t + 2, :, :].rearrange("p t m j -> p (t m j)"),
                )
            return codes, scales

        def product(out, weight, t, words, scales):
            codes, weight_scales = weight
            nc.tensor.matmul_mx(
                out,
                lhsT=codes[:, t, :].bitcast(FP8X4),
                lhsT_scale=weight_scales[:, t, :],
                rhs=words.bitcast(FP8X4),
                rhs_scale=scales,
                start=True,
                stop=True,
            )

        def entries(lst, h):
            return lst[:, HALF * h // PER_COLUMN : HALF * (h + 1) // PER_COLUMN]

        def planes_of(ap):
            return ap.rearrange("p t (c i) -> p c t i", i=PACK)

        def words_of(ap):
            return ap.rearrange("p (c i) t -> p c t i", i=PACK)

        e_scale_table = cleared_scale_table("e_scale_table", e_scales)
        x_scale_table = cleared_scale_table("x_scale_table", x_scales)
        old_list = load_list("old_list", old1)
        u = keep.tile([P, PACK], F32, name="u")
        nc.sync.dma_start(u[:], unit.rearrange("(p t) o -> p (t o)", t=PACK))
        e_word_table = load_words("e_word_table", e_words)
        w2_first = load_weight_half("w2_first", w2, 0)
        load_scales(e_scale_table, e_scales, 0)
        w2_second = load_weight_half("w2_second", w2, 1)
        offs_list = load_list("offs_list", offs)
        w1_first = load_weight_half("w1_first", w1, 0)
        load_scales(x_scale_table, x_scales, X_PLANE)
        w1_second = load_weight_half("w1_second", w1, 1)
        org_list = load_list("org_list", org)
        x_word_table = load_words("x_word_table", x_words)
        sib_list = load_list("sib_list", sib)
        w3_first = load_weight_half("w3_first", w3, 0)
        w3_second = load_weight_half("w3_second", w3, 1)

        e_picked_words = keep.tile([P, S], U32, name="e_picked_words", align_bytes=64)
        nc.vector.tensor_copy(e_picked_words[:], e_word_table[:].indirect(old_list[:]))
        e_picked_scales = keep.tile([P, S], U8, name="e_picked_scales", align_bytes=64)
        nc.vector.tensor_copy(e_picked_scales[:], e_scale_table[:].indirect(old_list[:]))
        w2_staged = keep.tile([P, PACK, P, PACK], BF16, name="w2_staged", align_bytes=64)
        nc.scalar.copy(*dealt(w2_staged, w2_first, 0))
        dst, src = dealt(w2_staged, w2_second, 1)
        nc.scalar.copy(dst[:, W2_VECTOR_M:M_HALF], src[:, W2_VECTOR_M:M_HALF])
        nc.vector.tensor_copy(dst[:, 0:W2_VECTOR_M], src[:, 0:W2_VECTOR_M])
        w2_mx = quantize_weight("w2", w2_staged)

        eou = keep.tile([P, PACK, S], F32, name="eou")
        yeu = []
        for t in range(PACK):
            bank = psum.tile([P, S], F32, name="bank%d" % t)
            product(bank[:], w2_mx, t, e_picked_words[:], e_picked_scales[:])
            yeu.append(keep.tile([P, S], F32, name="yeu%d" % t))
            nc.scalar.activation(yeu[t][:], bank[:], COPY, scale=u[:, t : t + 1])
        for t in range(PACK):
            for h in range(2):
                picked = yeu[t][:].indirect(entries(org_list, h))
                if t == 0:
                    nc.vector.tensor_copy(eou[:, t, HALF * h : HALF * (h + 1)], picked)
                else:
                    nc.scalar.activation(eou[:, t, HALF * h : HALF * (h + 1)], picked, COPY)

        y_gain = keep.tile([P, PACK], F32, name="y_gain")
        nc.vector.tensor_scalar(y_gain[:], u[:], -1.0 / LOSS, None, MULT)
        u_is_zero = keep.tile([P, PACK], F32, name="u_is_zero")
        nc.vector.tensor_scalar(u_is_zero[:], u[:], 0.0, None, IS_EQUAL)
        divisor = keep.tile([P, PACK], F32, name="divisor")
        nc.vector.scalar_tensor_tensor(divisor[:], u[:], 1.0 / (LOSS * LOSS), u_is_zero[:], MULT, ADD)
        prod_gain = keep.tile([P, PACK], F32, name="prod_gain")
        nc.vector.reciprocal(prod_gain[:], divisor[:])

        x_picked_scales = keep.tile([P, S], U8, name="x_picked_scales", align_bytes=64)
        nc.vector.tensor_copy(x_picked_scales[:], x_scale_table[:].indirect(offs_list[:]))
        x_picked_words = keep.tile([P, S], U32, name="x_picked_words", align_bytes=64)
        nc.vector.tensor_copy(x_picked_words[:], x_word_table[:].indirect(offs_list[:]))
        w1_staged = keep.tile([P, PACK, P, PACK], BF16, name="w1_staged", align_bytes=64)
        nc.vector.tensor_copy(*dealt(w1_staged, w1_first, 0))
        round_on_gpsimd(*dealt(w1_staged, w1_second, 1))
        w1_mx = quantize_weight("w1", w1_staged)

        w3_staged = keep.tile([P, PACK, P, PACK], BF16, name="w3_staged", tag="x_word_table", align_bytes=64)
        nc.vector.tensor_copy(*dealt(w3_staged, w3_first, 0))
        d = keep.tile([P, PACK, S], F32, name="d", tag="w3_first")
        for t in range(PACK):
            bank = psum.tile([P, S], F32, name="bank%d" % (PACK + t))
            product(bank[:], w1_mx, t, x_picked_words[:], x_picked_scales[X_PLANE:P, :])
            nc.vector.scalar_tensor_tensor(d[:, t, :], bank[:], y_gain[:, t : t + 1], eou[:, t, :], MULT, ADD)
        round_on_gpsimd(*dealt(w3_staged, w3_second, 1))
        w3_mx = quantize_weight("w3", w3_staged)

        out_rows = out_0.rearrange("(p t) j -> p t j", t=PACK)
        out_words = out_1[0].rearrange("p n r -> p (n r)").bitcast(I32)
        out_scales = keep.tile([P, S], U8, name="out_scales", align_bytes=64)
        for h in range(2):
            half_cols = slice(HALF * h, HALF * (h + 1))
            prod = keep.tile([P, PACK, HALF], F32, name="prod%d" % h, tag="x_word_table" if h == 0 else "prod_second", align_bytes=64)
            for t in range(PACK):
                sibling = ring.tile([P, HALF], F32, name="sibling")
                nc.scalar.activation(sibling[:], d[:, t, :].indirect(entries(sib_list, h)), COPY)
                nc.vector.scalar_tensor_tensor(prod[:, t, :], d[:, t, half_cols], prod_gain[:, t : t + 1], sibling[:], MULT, MULT)

            for step in range(2 * h, 2 * h + 2):
                cols = slice(QUARTER * step, QUARTER * (step + 1))
                cols_in_half = slice(cols.start - half_cols.start, cols.stop - half_cols.start)
                hid = keep.tile([P, QUARTER, PACK], BF16, name="hid", align_bytes=64)
                nc.vector.tensor_tensor(words_of(hid[:]), planes_of(prod[:, :, cols_in_half]), planes_of(eou[:, :, cols]), ADD)
                hid_codes = keep.tile([P, QUARTER], U32, name="hid_codes%d" % step, align_bytes=64)
                hid_scales = keep.tile([P, QUARTER], U8, name="hid_scales%d" % step, align_bytes=64)
                nc.vector.quantize_mx(out=hid_codes[:].bitcast(FP8X4), scales=hid_scales[:], in_=hid[:].rearrange("p n t -> p (n t)"))

                result = keep.tile([P, PACK, QUARTER], F32, name="result%d" % step)
                for pair in range(2):
                    bank = psum.tile([P, 2, QUARTER], F32, name="bank%d" % ((2 * step + pair) % PACK))
                    for v in range(2):
                        product(bank[:, v, :], w3_mx, 2 * pair + v, hid_codes[:], hid_scales[:])
                    nc.scalar.copy(result[:, 2 * pair : 2 * pair + 2, :], bank[:])
                nc.sync.dma_start(out_rows[:, :, cols], result[:])

                rounded = keep.tile([P, QUARTER, PACK], BF16, name="rounded%d" % step, align_bytes=64)
                round_result = nc.scalar.copy if h == 0 else nc.vector.tensor_copy
                round_result(words_of(rounded[:]), planes_of(result[:]))
                result_codes = keep.tile([P, QUARTER], U32, name="result_codes%d" % step, align_bytes=64)
                nc.vector.quantize_mx(out=result_codes[:].bitcast(FP8X4), scales=out_scales[:, cols], in_=rounded[:].rearrange("p n t -> p (n t)"))
                nc.sync.dma_start(out_words[:, cols], result_codes[:].bitcast(I32))

        for r in range(PACK):
            queue = nc.sync if r % 2 == 0 else nc.scalar
            queue.dma_start(out_2[0, r:SCALE_ROWS:PACK, :].bitcast(I32), out_scales[r:P:QUADRANT, :].bitcast(I32))
